import numpy as np
import ml_dtypes


def mxq(x, axis, fmt="e4m3"):
    dtype, down = {"e4m3": (ml_dtypes.float8_e4m3fn, 7), "e5m2": (ml_dtypes.float8_e5m2, 14)}[fmt]
    v = np.moveaxis(np.asarray(x, np.float32).astype(ml_dtypes.bfloat16).astype(np.float64), axis, -1)
    blocks = v.reshape(v.shape[:-1] + (-1, 32))
    amax = np.abs(blocks).max(-1, keepdims=True)
    byte = np.maximum(np.where(amax > 0, np.frexp(amax)[1] - 1 + 127, 0) - down, 1)
    scale = np.exp2(byte - 127.0)
    codes = (blocks / scale).astype(np.float32).astype(dtype).astype(np.float64)
    return np.moveaxis((codes * scale).reshape(v.shape), -1, axis)


WIDE = False


def mx_kscale(k):
    if not WIDE:
        return np.ones(k)
    levels = np.array([10, -10, 5, -5, 0])
    if k % 512:
        return np.exp2(np.random.permutation(np.resize(levels, k // 32))).repeat(32)
    a = np.empty((k // 512, 16))
    for p in range(k // 512):
        a[p, :8] = np.random.permutation(np.resize(levels, 8))
        for g in range(8):
            far = levels[np.abs(levels - a[p, g]) >= 10]
            a[p, g + 8] = far[np.random.randint(len(far))]
    return np.exp2(a.ravel()).repeat(32)


BF16 = ml_dtypes.bfloat16


def bf(x):
    return np.asarray(x, np.float32).astype(BF16)


def f64(x):
    return np.asarray(x).astype(np.float64)


E2M1 = np.array([0.0, 0.5, 1.0, 1.5, 2.0, 3.0, 4.0, 6.0, -0.0, -0.5, -1.0, -1.5, -2.0, -3.0, -4.0, -6.0])


def pack_weight(w, fmt):
    k, n = w.shape
    w = f64(bf(w)).reshape(k // 32, 32, n)
    amax = np.abs(w).max(1)
    if fmt == "e4m3":
        byte = np.frexp(amax)[1] - 1 + 127 - 7
    else:
        mant, ex = np.frexp(amax / 6.0)
        byte = np.where(mant > 0.5, ex, ex - 1) + 127
    byte = np.clip(np.where(amax > 0, byte, 1), 1, 254)
    scaled = (w * np.exp2(127.0 - byte)[:, None, :]).reshape(k, n).astype(np.float32)
    by_word = np.ascontiguousarray(scaled.reshape(k // 512, 128, 4, n).transpose(0, 1, 3, 2))
    if fmt == "e4m3":
        words = by_word.astype(ml_dtypes.float8_e4m3fn).view(np.uint8)
    else:
        c = by_word.astype(ml_dtypes.float4_e2m1fn).view(np.uint8) & 0xF
        words = c[..., 0::2] | (c[..., 1::2] << 4)
    return np.ascontiguousarray(words), np.ascontiguousarray(byte.astype(np.uint8).reshape(k // 512, 16, n))


def unpack_weight(words, scales, fmt):
    g, p, n, _ = words.shape
    if fmt == "e4m3":
        vals = np.ascontiguousarray(words).view(ml_dtypes.float8_e4m3fn).astype(np.float64)
    else:
        nib = np.empty((g, p, n, 4), np.uint8)
        nib[..., 0::2] = words & 0xF
        nib[..., 1::2] = words >> 4
        vals = E2M1[nib]
    vals = vals * np.repeat(np.exp2(scales.astype(np.float64) - 127.0), 8, axis=1)[..., None]
    return vals.transpose(0, 1, 3, 2).reshape(g * 512, n)
def pack4(w):
    words, scales = pack_weight(w, "e2m1")
    return words.reshape(words.shape[0], 128, -1), scales


def unpack4(words, scales):
    return unpack_weight(words.reshape(words.shape[0], 128, -1, 2), scales, "e2m1")


def planes(Y):
    n, m = Y.shape
    b = f64(bf(Y)).reshape(n // 32, 32, m)
    amax = np.abs(b).max(1)
    byte = np.clip(np.where(amax > 0, np.frexp(amax)[1] - 1 + 127 - 7, 1), 1, 254)
    codes = (b * np.exp2(127.0 - byte)[:, None, :]).reshape(n, m).astype(np.float32).astype(ml_dtypes.float8_e4m3fn).view(np.uint8)
    words = codes.reshape(n // 512, 128, 4, m).transpose(0, 1, 3, 2)
    return np.ascontiguousarray(words), np.ascontiguousarray(byte.astype(np.uint8).reshape(n // 512, 16, m))


C, R, S = 4, 1024, 512
T_LEFT, T_RIGHT, T_STEM = 0.5, 0.8, 0.6
RATES = np.linspace(0.4, 1.6, C)


def substitution(length):
    stay = np.exp(-RATES * length)[:, None, None]
    jump = np.exp(np.random.randn(C, S, S))
    jump = jump / jump.sum(axis=1, keepdims=True)
    return stay * np.eye(S) + (1.0 - stay) * jump


def setup_inputs():
    sl = mx_kscale(C * S).reshape(C, S)
    sr = mx_kscale(C * S).reshape(C, S)
    t = mx_kscale(C * S).reshape(C, S)
    left = np.exp(0.6 * np.random.randn(C, R, S)) / sl[:, None, :]
    right = np.exp(0.6 * np.random.randn(C, R, S)) / sr[:, None, :]
    wl = substitution(T_LEFT) * sl[:, :, None]
    wr = substitution(T_RIGHT) * sr[:, :, None] * t[:, None, :]
    wu = substitution(T_STEM) / t[:, :, None]
    left_words, left_scales = pack4(wl.reshape(C * S, S))
    right_words, right_scales = pack4(wr.reshape(C * S, S))
    stem_words, stem_scales = pack4(wu.reshape(C * S, S))
    sister = np.exp(0.8 * np.random.randn(S) + 0.3 * np.random.randn(C, R, S) - 0.4)
    rescale = np.exp(0.3 * np.random.randn(R))
    return {"left": bf(left), "right": bf(right),
            "left_words": left_words, "left_scales": left_scales,
            "right_words": right_words, "right_scales": right_scales,
            "stem_words": stem_words, "stem_scales": stem_scales,
            "sister": bf(sister), "rescale": bf(rescale)}


def reference(left, right, left_words, left_scales, right_words, right_scales, stem_words, stem_scales, sister, rescale):
    wl = unpack4(left_words, left_scales).reshape(C, S, S)
    wr = unpack4(right_words, right_scales).reshape(C, S, S)
    wu = unpack4(stem_words, stem_scales).reshape(C, S, S)
    a = mxq(f64(left), 2) @ wl
    b = mxq(f64(right), 2) @ wr
    node = a * b
    up = mxq(node, 2) @ wu
    y = up * f64(sister) * f64(rescale)[None, :, None]
    Y = y.reshape(C * R, S).T
    words, scales = planes(Y)
    return y, words, scales

@@ -1,0 +1,397 @@
+from contextlib import ExitStack
+
+import concourse.mybir as mybir
+from concourse.masks import make_identity
+
+C, R, S = 4, 1024, 512
+FLOPS = 3 * 2 * C * R * S * S
+
+F32 = mybir.dt.float32
+BF16 = mybir.dt.bfloat16
+I32 = mybir.dt.int32
+U32 = mybir.dt.uint32
+U8 = mybir.dt.uint8
+FP8X4 = mybir.dt.float8_e4m3fn_x4
+FP4X4 = mybir.dt.float4_e2m1fn_x4
+MULT = mybir.AluOpType.mult
+ADD = mybir.AluOpType.add
+
+P = 128
+ROWS = 4
+GROUP = P * ROWS
+GROUPS = C * R // GROUP
+PER_CAT = R // GROUP
+PAIR = 2
+STEPS = GROUPS * ROWS // PAIR
+WORDS = S // 2
+BANKS = 8
+SMALL_HEAD = 2
+SMALL_TAIL = 4
+LAG_N, LAG_U, LAG_Y = 1, 2, 4
+SLOTS = 3
+LEAD = 2
+LATE = 4
+TAILCONV = ("pool", "act", "pool", "dve")
+
+
+def tile_pruning_rate_categories_k7_kernel(
+    tc, left, right, left_words, left_scales, right_words, right_scales,
+    stem_words, stem_scales, sister, rescale, out_0, out_1, out_2,
+):
+    nc = tc.nc
+
+    groups = []
+    site = 0
+    while site < C * R:
+        small = site < SMALL_HEAD * PAIR * P or site >= C * R - SMALL_TAIL * PAIR * P
+        n = PAIR if small else ROWS
+        groups.append((site, n))
+        site = site + n * P
+    steps = [(g, j0) for g in range(len(groups)) for j0 in range(0, groups[g][1], PAIR)]
+
+    def cat(g):
+        return groups[g][0] // R
+
+    def by_group(x, g):
+        site0, n = groups[g]
+        return x[site0 // R, site0 % R : site0 % R + n * P, :].rearrange("(p j) k -> p j k", j=n)
+
+    with ExitStack() as ctx:
+        keep = ctx.enter_context(tc.tile_pool(name="keep", bufs=1))
+        work = ctx.enter_context(tc.tile_pool(name="work", bufs=3))
+        outs = ctx.enter_context(tc.tile_pool(name="outs", bufs=4))
+        psum = ctx.enter_context(tc.psum_pool(name="psum", bufs=1))
+        ctx.enter_context(tc.manual_schedule())
+
+        uses = []
+
+        def bank():
+            tag = "bank%d" % (len(uses) % BANKS)
+            uses.append(tag)
+            return psum.tile([P, S], F32, name=tag, tag=tag)
+
+        planes = {}
+        for nm in ("right", "left", "stem"):
+            planes[nm] = keep.tile([P, C, S], U8, name="plane_" + nm, align_bytes=64)
+            nc.vector.memset(planes[nm][:].bitcast(I32), 0)
+
+        ident = keep.tile([P, P], F32)
+        make_identity(nc, ident[:])
+
+        def load_scales(queue, nm, src):
+            for q in range(4):
+                queue.dma_start(
+                    out=planes[nm][32 * q : 32 * q + 4, :, :].bitcast(I32),
+                    in_=src[:, 4 * q : 4 * q + 4, :].rearrange("c r n -> r c n").bitcast(I32),
+                )
+
+        weights = {}
+
+        def load_words(nm, src, c0, c1):
+            w = keep.tile([P, c1 - c0, 2 * S], U8, name="w_%s_%d" % (nm, c0), align_bytes=64)
+            nc.sync.dma_start(out=w[:].bitcast(I32), in_=src[c0:c1].rearrange("c p n -> p c n").bitcast(I32))
+            for c in range(c0, c1):
+                weights[nm, c] = w[:, c - c0, :]
+
+        rows = {}
+
+        def load_rows(nm, src, g):
+            t = keep.tile([P, groups[g][1], S], BF16, name="x_%s_%d" % (nm, g))
+            nc.sync.dma_start(out=t[:], in_=by_group(src, g))
+            rows[nm, g] = t
+
+        factor = {}
+
+        def load_factor(n):
+            factor[n] = keep.tile([P, R // (n * P), n], BF16, name="factor_%d" % n)
+            nc.sync.dma_start(out=factor[n][:], in_=rescale.rearrange("(h p j) -> p h j", p=P, j=n))
+
+        load_rows("right", right, 0)
+        load_rows("left", left, 0)
+        load_scales(nc.sync, "right", right_scales)
+        load_words("right", right_words, 0, 1)
+        load_words("left", left_words, 0, 1)
+        load_rows("right", right, 1)
+        load_rows("left", left, 1)
+        load_scales(nc.sync, "left", left_scales)
+        load_rows("right", right, 2)
+        load_rows("left", left, 2)
+        load_words("stem", stem_words, 0, 1)
+        load_scales(nc.sync, "stem", stem_scales)
+        load_rows("right", right, 3)
+        load_rows("left", left, 3)
+        load_factor(PAIR)
+        load_rows("sister", sister, 0)
+        load_words("right", right_words, 1, C)
+        load_words("left", left_words, 1, C)
+        load_rows("sister", sister, 1)
+        load_factor(ROWS)
+        for g in range(4, len(groups)):
+            load_rows("right", right, g)
+            load_rows("left", left, g)
+            load_rows("sister", sister, g - 2)
+            if g == 4:
+                load_words("stem", stem_words, 1, C)
+        load_rows("sister", sister, len(groups) - 2)
+        load_rows("sister", sister, len(groups) - 1)
+
+        y_scales = keep.tile([P, C * R], U8, align_bytes=64)
+
+        st = {}
+
+        def sorted_pairs(ap):
+            return ap.rearrange("p (m u e) -> p u m e", u=2, e=2)
+
+        def as_sorted(ap):
+            return ap.rearrange("p (u m e) -> p u m e", u=2, e=2)
+
+        def turn_inputs(s):
+            g, j0 = steps[s]
+            for nm in ("right", "left"):
+                b = bank()
+                for j in range(PAIR):
+                    words = rows[nm, g][:, j0 + j, :].bitcast(F32)
+                    for u in range(2):
+                        nc.tensor.transpose(b[:, (2 * j + u) * P : (2 * j + u + 1) * P], words[:, u:WORDS:2], ident[:])
+                st["t_" + nm, s] = b
+
+        def turn_sorted(nm, s):
+            b = bank()
+            for j in range(PAIR):
+                for u in range(2):
+                    nc.tensor.transpose(b[:, (2 * j + u) * P : (2 * j + u + 1) * P], st[nm, s, j][:, u, :], ident[:])
+            st["t_" + nm, s] = b
+
+        def out_of_bank(dst, b):
+            nc.scalar.copy(
+                out=dst.bitcast(F32).rearrange("p (j r u) -> p j r u", j=PAIR, u=2),
+                in_=b[:].rearrange("p (j u r) -> p j r u", j=PAIR, u=2),
+            )
+
+        def copy_inputs(s):
+            xin = work.tile([P, 2 * PAIR * S], BF16, name="xin", tag="slot%d" % (s % SLOTS), bufs=1, align_bytes=64)
+            out_of_bank(xin[:, : PAIR * S], st["t_right", s])
+            out_of_bank(xin[:, PAIR * S :], st["t_left", s])
+            st["xin", s] = xin
+
+        def copy_node(s):
+            nin = work.tile([P, PAIR * S], BF16, align_bytes=64)
+            out_of_bank(nin[:], st["t_node", s])
+            st["nin", s] = nin
+
+        def copy_y(s):
+            g, j0 = steps[s]
+            n = groups[g][1]
+            if j0 == 0:
+                yin = work.tile([P, n * S], BF16, align_bytes=64)
+                st["yin", g] = yin
+            nc.scalar.copy(
+                out=st["yin", g][:].bitcast(F32).rearrange("p (r w) -> p r w", w=2 * n)[:, :, 2 * j0 : 2 * (j0 + PAIR)],
+                in_=st["t_ybf", s][:].rearrange("p (w r) -> p r w", r=P),
+            )
+
+        def quantize(pool, nm, src, width):
+            codes = pool.tile([P, width], U32, name=nm + "_codes", align_bytes=64)
+            scales = pool.tile([P, width], U8, name=nm + "_scales", align_bytes=64)
+            nc.vector.quantize_mx(out=codes[:].bitcast(FP8X4), scales=scales[:], in_=src[:])
+            return codes, scales
+
+        def product(q, col, nm, c):
+            codes, scales = q
+            b = bank()
+            nc.tensor.matmul_mx(
+                out=b[:],
+                lhsT=codes[:, col * P : (col + 1) * P].bitcast(FP8X4),
+                lhsT_scale=scales[:, col * P : (col + 1) * P],
+                rhs=weights[nm, c].bitcast(FP4X4),
+                rhs_scale=planes[nm][:, c, :],
+                start=True,
+                stop=True,
+            )
+            return b
+
+        def stem_products(s):
+            for j in range(PAIR):
+                st["up", s, j] = product(st["nq", s], j, "stem", cat(steps[s][0]))
+
+        def child_products(s):
+            c = cat(steps[s][0])
+            for j in range(PAIR):
+                st["b", s, j] = product(st["xq", s], j, "right", c)
+            for j in range(PAIR):
+                st["a", s, j] = product(st["xq", s], PAIR + j, "left", c)
+
+        def copy_b(s):
+            for j in range(PAIR):
+                b_sb = outs.tile([P, S], F32)
+                nc.scalar.copy(out=as_sorted(b_sb[:]), in_=sorted_pairs(st["b", s, j][:]))
+                st["b_sb", s, j] = b_sb
+
+        def node_product(s):
+            for j in range(PAIR):
+                node = outs.tile([P, S], BF16, bufs=2 * LAG_N + 2)
+                nc.vector.tensor_tensor(
+                    out=as_sorted(node[:]), in0=sorted_pairs(st["a", s, j][:]), in1=as_sorted(st["b_sb", s, j][:]), op=MULT
+                )
+                st["node", s, j] = node[:].bitcast(F32).rearrange("p (u m) -> p u m", u=2)
+
+        def result(s):
+            g, j0 = steps[s]
+            site0, n = groups[g]
+            if j0 == 0:
+                y = outs.tile([P, n, S], F32)
+                st["y", g] = y
+            for j in range(PAIR):
+                nc.vector.scalar_tensor_tensor(
+                    out=st["y", g][:, j0 + j, :],
+                    in0=st["up", s, j][:],
+                    scalar=factor[n][:, site0 % R // (n * P), j0 + j : j0 + j + 1],
+                    in1=rows["sister", g][:, j0 + j, :],
+                    op0=MULT,
+                    op1=MULT,
+                )
+            if j0 + PAIR == n:
+                nc.sync.dma_start(out=by_group(out_0, g), in_=st["y", g][:])
+
+        def round_pair(s, slot):
+            g, j0 = steps[s]
+            ybf = work.tile([P, PAIR * S], BF16, name="ybf", tag="slot%d" % (slot % SLOTS), bufs=1, align_bytes=64)
+            nc.gpsimd.tensor_scalar(
+                out=ybf[:].rearrange("p (u w e) -> p u w e", u=2, e=2),
+                in0=st["y", g][:, j0 : j0 + PAIR, :].rearrange("p j (m u e) -> p u (j m) e", u=2, e=2),
+                scalar1=1.0, scalar2=0.0, op0=MULT, op1=ADD,
+            )
+            words = ybf[:].bitcast(F32).rearrange("p (u j m) -> p j u m", u=2, j=PAIR)
+            for j in range(PAIR):
+                st["ybf", s, j] = words[:, j]
+
+        def round_tiles(s, engine):
+            g, j0 = steps[s]
+            for j in range(PAIR):
+                ytile = outs.tile([P, S], BF16)
+                src = sorted_pairs(st["y", g][:, j0 + j, :])
+                if engine == "act":
+                    nc.scalar.copy(out=as_sorted(ytile[:]), in_=src)
+                elif engine == "pool":
+                    nc.gpsimd.tensor_scalar(out=as_sorted(ytile[:]), in0=src, scalar1=1.0, scalar2=0.0, op0=MULT, op1=ADD)
+                else:
+                    nc.vector.tensor_copy(out=as_sorted(ytile[:]), in_=src)
+                st["ybf", s, j] = ytile[:].bitcast(F32).rearrange("p (u m) -> p u m", u=2)
+
+        def store_scales(lo, hi):
+            for q in range(4):
+                nc.sync.dma_start(
+                    out=out_2[0, 4 * q : 4 * q + 4, lo:hi].bitcast(I32),
+                    in_=y_scales[32 * q : 32 * q + 4, lo:hi].bitcast(I32),
+                )
+
+        def planes_out(g):
+            site0, n = groups[g]
+            y_codes = outs.tile([P, n * P], U32, align_bytes=64)
+            cols = slice(site0, site0 + n * P)
+            nc.vector.quantize_mx(out=y_codes[:].bitcast(FP8X4), scales=y_scales[:, cols], in_=st["yin", g][:])
+            nc.sync.dma_start(
+                out=out_1[0, :, cols, :].rearrange("p m t -> p (m t)").bitcast(I32), in_=y_codes[:].bitcast(I32)
+            )
+            if g == len(groups) - 1 - LATE:
+                store_scales(0, cols.stop)
+            if g == len(groups) - 1:
+                store_scales(groups[-LATE][0], cols.stop)
+
+        def live(s):
+            return 0 <= s < STEPS
+
+        def quantize_node(s):
+            st["nq", s] = quantize(work, "node", st["nin", s], PAIR * P)
+
+        def quantize_inputs(s):
+            st["xq", s] = quantize(work, "child", st["xin", s], 2 * PAIR * P)
+
+        def planes_if_whole(s):
+            g, j0 = steps[s]
+            if j0 + PAIR == groups[g][1]:
+                planes_out(g)
+
+        def turns(fresh, results, nodes):
+            for s in fresh:
+                turn_inputs(s)
+            for s in results:
+                turn_sorted("ybf", s)
+            for s in nodes:
+                turn_sorted("node", s)
+            for s in fresh:
+                copy_inputs(s)
+            for s in results:
+                copy_y(s)
+            for s in nodes:
+                copy_node(s)
+
+        def some(s):
+            return [s] if live(s) else []
+
+        for s in range(LEAD):
+            turns([s], [], [])
+            quantize_inputs(s)
+        for s in range(STEPS - LEAD):
+            if s > 0:
+                turns([s + LEAD], some(s - LAG_Y), some(s - LAG_N))
+            for r in some(s - LAG_U):
+                stem_products(r)
+            child_products(s)
+            copy_b(s)
+            if s == 0:
+                turns([s + LEAD], [], [])
+            for r in some(s - LAG_U):
+                result(r)
+            node_product(s)
+            for r in some(s - LAG_N):
+                quantize_node(r)
+            for r in some(s - LAG_Y):
+                planes_if_whole(r)
+            quantize_inputs(s + LEAD)
+            for r in some(s - LAG_U):
+                round_pair(r, s + LEAD)
+
+        def turn_node(s):
+            turn_sorted("node", s)
+            copy_node(s)
+
+        def turn_result(s):
+            turn_sorted("ybf", s)
+            copy_y(s)
+
+        last = STEPS - 1
+        child_products(last - 1)
+        copy_b(last - 1)
+        stem_products(last - 3)
+        turn_node(last - 2)
+        turn_result(last - 5)
+        node_product(last - 1)
+        child_products(last)
+        copy_b(last)
+        quantize_node(last - 2)
+        result(last - 3)
+        turn_node(last - 1)
+        turn_result(last - 4)
+        round_tiles(last - 3, TAILCONV[0])
+        stem_products(last - 2)
+        node_product(last)
+        turn_node(last)
+        quantize_node(last - 1)
+        stem_products(last - 1)
+        planes_if_whole(last - 4)
+        result(last - 2)
+        turn_result(last - 3)
+        round_tiles(last - 2, TAILCONV[1])
+        quantize_node(last)
+        stem_products(last)
+        result(last - 1)
+        turn_result(last - 2)
+        round_tiles(last - 1, TAILCONV[2])
+        result(last)
+        turn_result(last - 1)
+        planes_if_whole(last - 3)
+        round_tiles(last, TAILCONV[3])
+        turn_result(last)
+        for s in range(last - 2, STEPS):
+            planes_if_whole(s)

@@ -30,8 +30,9 @@ SMALL_TAIL = 4
 LAG_N, LAG_U, LAG_Y = 1, 2, 4
 SLOTS = 3
 LEAD = 2
-LATE = 4
 TAILCONV = ("pool", "act", "pool", "dve")
+AHEAD = 6
+SISTER_AHEAD = 3
 
 
 def tile_pruning_rate_categories_k7_kernel(
@@ -48,6 +49,8 @@ def tile_pruning_rate_categories_k7_kernel(
         groups.append((site, n))
         site = site + n * P
     steps = [(g, j0) for g in range(len(groups)) for j0 in range(0, groups[g][1], PAIR)]
+
+    first_step = [steps.index((g, 0)) for g in range(len(groups))]
 
     def cat(g):
         return groups[g][0] // R
@@ -79,10 +82,10 @@ def tile_pruning_rate_categories_k7_kernel(
         make_identity(nc, ident[:])
 
         def load_scales(queue, nm, src):
-            for q in range(4):
+            for r in range(4):
                 queue.dma_start(
-                    out=planes[nm][32 * q : 32 * q + 4, :, :].bitcast(I32),
-                    in_=src[:, 4 * q : 4 * q + 4, :].rearrange("c r n -> r c n").bitcast(I32),
+                    out=planes[nm][r:P:32, :, :].bitcast(I32),
+                    in_=src[:, r:16:4, :].rearrange("c q n -> q c n").bitcast(I32),
                 )
 
         weights = {}
@@ -124,16 +127,19 @@ def tile_pruning_rate_categories_k7_kernel(
         load_rows("sister", sister, 0)
         load_words("right", right_words, 1, C)
         load_words("left", left_words, 1, C)
-        load_rows("sister", sister, 1)
         load_factor(ROWS)
-        for g in range(4, len(groups)):
-            load_rows("right", right, g)
-            load_rows("left", left, g)
-            load_rows("sister", sister, g - 2)
-            if g == 4:
-                load_words("stem", stem_words, 1, C)
-        load_rows("sister", sister, len(groups) - 2)
-        load_rows("sister", sister, len(groups) - 1)
+        load_words("stem", stem_words, 1, C)
+
+        def load_ahead(s):
+            for g in range(len(groups)):
+                if first_step[g] == s + AHEAD and g > 3:
+                    load_rows("right", right, g)
+                    load_rows("left", left, g)
+                if first_step[g] == s + SISTER_AHEAD and g > 0:
+                    load_rows("sister", sister, g)
+
+        for s in range(-AHEAD, 0):
+            load_ahead(s)
 
         y_scales = keep.tile([P, C * R], U8, align_bytes=64)
 
@@ -279,10 +285,11 @@ def tile_pruning_rate_categories_k7_kernel(
                 st["ybf", s, j] = ytile[:].bitcast(F32).rearrange("p (u m) -> p u m", u=2)
 
         def store_scales(lo, hi):
-            for q in range(4):
-                nc.sync.dma_start(
-                    out=out_2[0, 4 * q : 4 * q + 4, lo:hi].bitcast(I32),
-                    in_=y_scales[32 * q : 32 * q + 4, lo:hi].bitcast(I32),
+            for r in range(4):
+                queue = nc.scalar if hi == C * R and r % 2 else nc.sync
+                queue.dma_start(
+                    out=out_2[0, r:16:4, lo:hi].bitcast(I32),
+                    in_=y_scales[r:P:32, lo:hi].bitcast(I32),
                 )
 
         def planes_out(g):
@@ -293,10 +300,8 @@ def tile_pruning_rate_categories_k7_kernel(
             nc.sync.dma_start(
                 out=out_1[0, :, cols, :].rearrange("p m t -> p (m t)").bitcast(I32), in_=y_codes[:].bitcast(I32)
             )
-            if g == len(groups) - 1 - LATE:
-                store_scales(0, cols.stop)
-            if g == len(groups) - 1:
-                store_scales(groups[-LATE][0], cols.stop)
+            if cols.stop % R == 0:
+                store_scales(cols.stop - R, cols.stop)
 
         def live(s):
             return 0 <= s < STEPS
@@ -333,6 +338,7 @@ def tile_pruning_rate_categories_k7_kernel(
             turns([s], [], [])
             quantize_inputs(s)
         for s in range(STEPS - LEAD):
+            load_ahead(s)
             if s > 0:
                 turns([s + LEAD], some(s - LAG_Y), some(s - LAG_N))
             for r in some(s - LAG_U):

@@ -17,22 +17,29 @@ MULT = mybir.AluOpType.mult
 ADD = mybir.AluOpType.add
 
 P = 128
-ROWS = 4
-GROUP = P * ROWS
-GROUPS = C * R // GROUP
-PER_CAT = R // GROUP
-PAIR = 2
-STEPS = GROUPS * ROWS // PAIR
 WORDS = S // 2
+PAIR = 2
+STEPS = C * R // (PAIR * P)
 BANKS = 8
-SMALL_HEAD = 2
-SMALL_TAIL = 4
-LAG_N, LAG_U, LAG_Y = 1, 2, 4
-SLOTS = 3
-LEAD = 2
-TAILCONV = ("pool", "act", "pool", "dve")
-AHEAD = 6
-SISTER_AHEAD = 3
+SCALE_ROWS = 16
+QUADRANT = 32
+
+WIDE = 4
+NARROW_HEAD = 2
+NARROW_TAIL = 4
+
+INPUT_LEAD = 2
+NODE_TURN_LAG = 1
+NODE_QUANT_LAG = 2
+STEM_LAG = 3
+RESULT_TURN_LAG = 5
+PLANES_LAG = 6
+CHILD_PRELOAD = 6
+SISTER_PRELOAD = 2
+
+FIRST_GROUPS = 4
+ROW_BUFS = 5
+SHARED_SLOTS = 4
 
 
 def tile_pruning_rate_categories_k7_kernel(
@@ -44,360 +51,324 @@ def tile_pruning_rate_categories_k7_kernel(
     groups = []
     site = 0
     while site < C * R:
-        small = site < SMALL_HEAD * PAIR * P or site >= C * R - SMALL_TAIL * PAIR * P
-        n = PAIR if small else ROWS
-        groups.append((site, n))
-        site = site + n * P
+        narrow = site < NARROW_HEAD * PAIR * P or site >= C * R - NARROW_TAIL * PAIR * P
+        groups.append((site, PAIR if narrow else WIDE))
+        site = site + groups[-1][1] * P
     steps = [(g, j0) for g in range(len(groups)) for j0 in range(0, groups[g][1], PAIR)]
-
     first_step = [steps.index((g, 0)) for g in range(len(groups))]
 
-    def cat(g):
-        return groups[g][0] // R
+    def category(s):
+        return groups[steps[s][0]][0] // R
 
-    def by_group(x, g):
+    def group_rows(x, g):
         site0, n = groups[g]
         return x[site0 // R, site0 % R : site0 % R + n * P, :].rearrange("(p j) k -> p j k", j=n)
 
+    def if_step(s):
+        return [s] if 0 <= s < STEPS else []
+
     with ExitStack() as ctx:
         keep = ctx.enter_context(tc.tile_pool(name="keep", bufs=1))
-        work = ctx.enter_context(tc.tile_pool(name="work", bufs=3))
-        outs = ctx.enter_context(tc.tile_pool(name="outs", bufs=4))
+        work = ctx.enter_context(tc.tile_pool(name="work", bufs=4))
         psum = ctx.enter_context(tc.psum_pool(name="psum", bufs=1))
         ctx.enter_context(tc.manual_schedule())
 
-        uses = []
+        bank_uses = []
 
-        def bank():
-            tag = "bank%d" % (len(uses) % BANKS)
-            uses.append(tag)
+        def next_bank():
+            tag = "bank%d" % (len(bank_uses) % BANKS)
+            bank_uses.append(tag)
             return psum.tile([P, S], F32, name=tag, tag=tag)
 
-        planes = {}
-        for nm in ("right", "left", "stem"):
-            planes[nm] = keep.tile([P, C, S], U8, name="plane_" + nm, align_bytes=64)
-            nc.vector.memset(planes[nm][:].bitcast(I32), 0)
+        weight_scales = {}
+        for branch in ("right", "left", "stem"):
+            weight_scales[branch] = keep.tile([P, C, S], U8, name="scales_" + branch, align_bytes=64)
+            nc.vector.memset(weight_scales[branch][:].bitcast(I32), 0)
 
         ident = keep.tile([P, P], F32)
         make_identity(nc, ident[:])
 
-        def load_scales(queue, nm, src):
+        def load_scales(branch, src):
             for r in range(4):
-                queue.dma_start(
-                    out=planes[nm][r:P:32, :, :].bitcast(I32),
-                    in_=src[:, r:16:4, :].rearrange("c q n -> q c n").bitcast(I32),
+                nc.sync.dma_start(
+                    out=weight_scales[branch][r:P:QUADRANT, :, :].bitcast(I32),
+                    in_=src[:, r:SCALE_ROWS:4, :].rearrange("c q n -> q c n").bitcast(I32),
                 )
 
-        weights = {}
+        weight_words = {}
 
-        def load_words(nm, src, c0, c1):
-            w = keep.tile([P, c1 - c0, 2 * S], U8, name="w_%s_%d" % (nm, c0), align_bytes=64)
+        def load_words(branch, src, c0, c1):
+            w = keep.tile([P, c1 - c0, 2 * S], U8, name="words_%s_%d" % (branch, c0), align_bytes=64)
             nc.sync.dma_start(out=w[:].bitcast(I32), in_=src[c0:c1].rearrange("c p n -> p c n").bitcast(I32))
             for c in range(c0, c1):
-                weights[nm, c] = w[:, c - c0, :]
+                weight_words[branch, c] = w[:, c - c0, :]
 
         rows = {}
 
-        def load_rows(nm, src, g):
-            t = keep.tile([P, groups[g][1], S], BF16, name="x_%s_%d" % (nm, g))
-            nc.sync.dma_start(out=t[:], in_=by_group(src, g))
-            rows[nm, g] = t
+        def load_rows(name, src, g):
+            rows[name, g] = work.tile([P, groups[g][1], S], BF16, name="rows_" + name, bufs=ROW_BUFS)
+            nc.sync.dma_start(out=rows[name, g][:], in_=group_rows(src, g))
 
-        factor = {}
+        def load_children(g):
+            load_rows("right", right, g)
+            load_rows("left", left, g)
 
-        def load_factor(n):
-            factor[n] = keep.tile([P, R // (n * P), n], BF16, name="factor_%d" % n)
-            nc.sync.dma_start(out=factor[n][:], in_=rescale.rearrange("(h p j) -> p h j", p=P, j=n))
+        site_factor = {}
 
-        load_rows("right", right, 0)
-        load_rows("left", left, 0)
-        load_scales(nc.sync, "right", right_scales)
+        def load_site_factor(n):
+            site_factor[n] = keep.tile([P, R // (n * P), n], BF16, name="site_factor_%d" % n)
+            nc.sync.dma_start(out=site_factor[n][:], in_=rescale.rearrange("(h p j) -> p h j", p=P, j=n))
+
+        def preload(s):
+            for g in range(len(groups)):
+                if g >= FIRST_GROUPS and first_step[g] == s + CHILD_PRELOAD:
+                    load_children(g)
+                if g > 0 and first_step[g] == s + SISTER_PRELOAD:
+                    load_rows("sister", sister, g)
+
+        load_children(0)
+        load_scales("right", right_scales)
         load_words("right", right_words, 0, 1)
         load_words("left", left_words, 0, 1)
-        load_rows("right", right, 1)
-        load_rows("left", left, 1)
-        load_scales(nc.sync, "left", left_scales)
-        load_rows("right", right, 2)
-        load_rows("left", left, 2)
+        load_children(1)
+        load_scales("left", left_scales)
+        load_children(2)
         load_words("stem", stem_words, 0, 1)
-        load_scales(nc.sync, "stem", stem_scales)
-        load_rows("right", right, 3)
-        load_rows("left", left, 3)
-        load_factor(PAIR)
+        load_scales("stem", stem_scales)
+        load_children(3)
+        load_site_factor(PAIR)
         load_rows("sister", sister, 0)
         load_words("right", right_words, 1, C)
         load_words("left", left_words, 1, C)
-        load_factor(ROWS)
+        load_site_factor(WIDE)
         load_words("stem", stem_words, 1, C)
+        for s in range(-CHILD_PRELOAD, 0):
+            preload(s)
 
-        def load_ahead(s):
-            for g in range(len(groups)):
-                if first_step[g] == s + AHEAD and g > 3:
-                    load_rows("right", right, g)
-                    load_rows("left", left, g)
-                if first_step[g] == s + SISTER_AHEAD and g > 0:
-                    load_rows("sister", sister, g)
-
-        for s in range(-AHEAD, 0):
-            load_ahead(s)
-
-        y_scales = keep.tile([P, C * R], U8, align_bytes=64)
-
-        st = {}
-
-        def sorted_pairs(ap):
+        def read_sorted(ap):
             return ap.rearrange("p (m u e) -> p u m e", u=2, e=2)
 
-        def as_sorted(ap):
+        def write_sorted(ap):
             return ap.rearrange("p (u m e) -> p u m e", u=2, e=2)
 
-        def turn_inputs(s):
-            g, j0 = steps[s]
-            for nm in ("right", "left"):
-                b = bank()
-                for j in range(PAIR):
-                    words = rows[nm, g][:, j0 + j, :].bitcast(F32)
-                    for u in range(2):
-                        nc.tensor.transpose(b[:, (2 * j + u) * P : (2 * j + u + 1) * P], words[:, u:WORDS:2], ident[:])
-                st["t_" + nm, s] = b
-
-        def turn_sorted(nm, s):
-            b = bank()
+        def turn(words_of):
+            b = next_bank()
             for j in range(PAIR):
                 for u in range(2):
-                    nc.tensor.transpose(b[:, (2 * j + u) * P : (2 * j + u + 1) * P], st[nm, s, j][:, u, :], ident[:])
-            st["t_" + nm, s] = b
+                    slot = PAIR * u + j
+                    nc.tensor.transpose(b[:, slot * P : (slot + 1) * P], words_of(j, u), ident[:])
+            return b
 
-        def out_of_bank(dst, b):
+        def interleave(dst, b):
             nc.scalar.copy(
-                out=dst.bitcast(F32).rearrange("p (j r u) -> p j r u", j=PAIR, u=2),
-                in_=b[:].rearrange("p (j u r) -> p j r u", j=PAIR, u=2),
+                out=dst.bitcast(F32).rearrange("p (c i u) -> p c u i", i=2, u=2),
+                in_=b[:].rearrange("p (u c i) -> p c u i", u=2, i=2),
             )
 
-        def copy_inputs(s):
-            xin = work.tile([P, 2 * PAIR * S], BF16, name="xin", tag="slot%d" % (s % SLOTS), bufs=1, align_bytes=64)
-            out_of_bank(xin[:, : PAIR * S], st["t_right", s])
-            out_of_bank(xin[:, PAIR * S :], st["t_left", s])
-            st["xin", s] = xin
+        def shared_slot(name, width, s):
+            return work.tile([P, width], BF16, name=name, tag="shared%d" % (s % SHARED_SLOTS), bufs=1, align_bytes=64)
 
-        def copy_node(s):
-            nin = work.tile([P, PAIR * S], BF16, align_bytes=64)
-            out_of_bank(nin[:], st["t_node", s])
-            st["nin", s] = nin
-
-        def copy_y(s):
-            g, j0 = steps[s]
-            n = groups[g][1]
-            if j0 == 0:
-                yin = work.tile([P, n * S], BF16, align_bytes=64)
-                st["yin", g] = yin
-            nc.scalar.copy(
-                out=st["yin", g][:].bitcast(F32).rearrange("p (r w) -> p r w", w=2 * n)[:, :, 2 * j0 : 2 * (j0 + PAIR)],
-                in_=st["t_ybf", s][:].rearrange("p (w r) -> p r w", r=P),
-            )
-
-        def quantize(pool, nm, src, width):
-            codes = pool.tile([P, width], U32, name=nm + "_codes", align_bytes=64)
-            scales = pool.tile([P, width], U8, name=nm + "_scales", align_bytes=64)
+        def quantize(name, src):
+            width = src.shape[1] // 4
+            codes = work.tile([P, width], U32, name=name + "_codes", align_bytes=64)
+            scales = work.tile([P, width], U8, name=name + "_scales", align_bytes=64)
             nc.vector.quantize_mx(out=codes[:].bitcast(FP8X4), scales=scales[:], in_=src[:])
             return codes, scales
 
-        def product(q, col, nm, c):
-            codes, scales = q
-            b = bank()
+        def product(quantized, slot, branch, c):
+            codes, scales = quantized
+            b = next_bank()
             nc.tensor.matmul_mx(
                 out=b[:],
-                lhsT=codes[:, col * P : (col + 1) * P].bitcast(FP8X4),
-                lhsT_scale=scales[:, col * P : (col + 1) * P],
-                rhs=weights[nm, c].bitcast(FP4X4),
-                rhs_scale=planes[nm][:, c, :],
+                lhsT=codes[:, slot * P : (slot + 1) * P].bitcast(FP8X4),
+                lhsT_scale=scales[:, slot * P : (slot + 1) * P],
+                rhs=weight_words[branch, c].bitcast(FP4X4),
+                rhs_scale=weight_scales[branch][:, c, :],
                 start=True,
                 stop=True,
             )
             return b
 
-        def stem_products(s):
-            for j in range(PAIR):
-                st["up", s, j] = product(st["nq", s], j, "stem", cat(steps[s][0]))
+        children_turned, children_mx, a_bank, b_bank, b_copy = {}, {}, {}, {}, {}
+        node_sorted, node_turned, node_mx, up_bank = {}, {}, {}, {}
+        y, y_sorted, y_turned = {}, {}, {}
+        y_scales = keep.tile([P, C * R], U8, align_bytes=64)
+
+        def turn_children(s):
+            g, j0 = steps[s]
+            banks = [
+                turn(lambda j, u: rows[name, g][:, j0 + j, :].bitcast(F32)[:, u:WORDS:2]) for name in ("right", "left")
+            ]
+            children_turned[s] = shared_slot("children_turned", 2 * PAIR * S, s)
+            for half in range(2):
+                interleave(children_turned[s][:, half * PAIR * S : (half + 1) * PAIR * S], banks[half])
+
+        def quantize_children(s):
+            children_mx[s] = quantize("children", children_turned[s])
 
         def child_products(s):
-            c = cat(steps[s][0])
             for j in range(PAIR):
-                st["b", s, j] = product(st["xq", s], j, "right", c)
+                b_bank[s, j] = product(children_mx[s], j, "right", category(s))
             for j in range(PAIR):
-                st["a", s, j] = product(st["xq", s], PAIR + j, "left", c)
+                a_bank[s, j] = product(children_mx[s], PAIR + j, "left", category(s))
 
         def copy_b(s):
             for j in range(PAIR):
-                b_sb = outs.tile([P, S], F32)
-                nc.scalar.copy(out=as_sorted(b_sb[:]), in_=sorted_pairs(st["b", s, j][:]))
-                st["b_sb", s, j] = b_sb
+                b_copy[s, j] = work.tile([P, S], F32, name="b_copy")
+                nc.scalar.copy(out=write_sorted(b_copy[s, j][:]), in_=read_sorted(b_bank[s, j][:]))
 
-        def node_product(s):
+        def multiply_children(s):
             for j in range(PAIR):
-                node = outs.tile([P, S], BF16, bufs=2 * LAG_N + 2)
+                node = work.tile([P, S], BF16)
                 nc.vector.tensor_tensor(
-                    out=as_sorted(node[:]), in0=sorted_pairs(st["a", s, j][:]), in1=as_sorted(st["b_sb", s, j][:]), op=MULT
+                    out=write_sorted(node[:]), in0=read_sorted(a_bank[s, j][:]), in1=write_sorted(b_copy[s, j][:]), op=MULT
                 )
-                st["node", s, j] = node[:].bitcast(F32).rearrange("p (u m) -> p u m", u=2)
+                node_sorted[s, j] = node[:].bitcast(F32).rearrange("p (u m) -> p u m", u=2)
+
+        def turn_node(s):
+            b = turn(lambda j, u: node_sorted[s, j][:, u, :])
+            node_turned[s] = work.tile([P, PAIR * S], BF16, name="node_turned", align_bytes=64)
+            interleave(node_turned[s][:], b)
+
+        def quantize_node(s):
+            node_mx[s] = quantize("node", node_turned[s])
+
+        def stem_products(s):
+            for j in range(PAIR):
+                up_bank[s, j] = product(node_mx[s], j, "stem", category(s))
 
         def result(s):
             g, j0 = steps[s]
             site0, n = groups[g]
             if j0 == 0:
-                y = outs.tile([P, n, S], F32)
-                st["y", g] = y
-            for j in range(PAIR):
+                y[g] = keep.tile([P, n, S], F32, name="y_%d" % g)
+            for j in range(j0, j0 + PAIR):
                 nc.vector.scalar_tensor_tensor(
-                    out=st["y", g][:, j0 + j, :],
-                    in0=st["up", s, j][:],
-                    scalar=factor[n][:, site0 % R // (n * P), j0 + j : j0 + j + 1],
-                    in1=rows["sister", g][:, j0 + j, :],
+                    out=y[g][:, j, :],
+                    in0=up_bank[s, j - j0][:],
+                    scalar=site_factor[n][:, site0 % R // (n * P), j : j + 1],
+                    in1=rows["sister", g][:, j, :],
                     op0=MULT,
                     op1=MULT,
                 )
             if j0 + PAIR == n:
-                nc.sync.dma_start(out=by_group(out_0, g), in_=st["y", g][:])
+                nc.sync.dma_start(out=group_rows(out_0, g), in_=y[g][:])
 
-        def round_pair(s, slot):
+        def round_on_gpsimd(s, slot_step):
             g, j0 = steps[s]
-            ybf = work.tile([P, PAIR * S], BF16, name="ybf", tag="slot%d" % (slot % SLOTS), bufs=1, align_bytes=64)
+            pair = shared_slot("y_pair", PAIR * S, slot_step)
             nc.gpsimd.tensor_scalar(
-                out=ybf[:].rearrange("p (u w e) -> p u w e", u=2, e=2),
-                in0=st["y", g][:, j0 : j0 + PAIR, :].rearrange("p j (m u e) -> p u (j m) e", u=2, e=2),
-                scalar1=1.0, scalar2=0.0, op0=MULT, op1=ADD,
+                out=pair[:].rearrange("p (u w e) -> p u w e", u=2, e=2),
+                in0=y[g][:, j0 : j0 + PAIR, :].rearrange("p j (m u e) -> p u (j m) e", u=2, e=2),
+                scalar1=1.0,
+                scalar2=0.0,
+                op0=MULT,
+                op1=ADD,
             )
-            words = ybf[:].bitcast(F32).rearrange("p (u j m) -> p j u m", u=2, j=PAIR)
             for j in range(PAIR):
-                st["ybf", s, j] = words[:, j]
+                y_sorted[s, j] = pair[:].bitcast(F32).rearrange("p (u j m) -> p j u m", u=2, j=PAIR)[:, j]
 
-        def round_tiles(s, engine):
+        def round_by_copy(s, copy):
             g, j0 = steps[s]
             for j in range(PAIR):
-                ytile = outs.tile([P, S], BF16)
-                src = sorted_pairs(st["y", g][:, j0 + j, :])
-                if engine == "act":
-                    nc.scalar.copy(out=as_sorted(ytile[:]), in_=src)
-                elif engine == "pool":
-                    nc.gpsimd.tensor_scalar(out=as_sorted(ytile[:]), in0=src, scalar1=1.0, scalar2=0.0, op0=MULT, op1=ADD)
-                else:
-                    nc.vector.tensor_copy(out=as_sorted(ytile[:]), in_=src)
-                st["ybf", s, j] = ytile[:].bitcast(F32).rearrange("p (u m) -> p u m", u=2)
-
-        def store_scales(lo, hi):
-            for r in range(4):
-                queue = nc.scalar if hi == C * R and r % 2 else nc.sync
-                queue.dma_start(
-                    out=out_2[0, r:16:4, lo:hi].bitcast(I32),
-                    in_=y_scales[r:P:32, lo:hi].bitcast(I32),
-                )
-
-        def planes_out(g):
-            site0, n = groups[g]
-            y_codes = outs.tile([P, n * P], U32, align_bytes=64)
-            cols = slice(site0, site0 + n * P)
-            nc.vector.quantize_mx(out=y_codes[:].bitcast(FP8X4), scales=y_scales[:, cols], in_=st["yin", g][:])
-            nc.sync.dma_start(
-                out=out_1[0, :, cols, :].rearrange("p m t -> p (m t)").bitcast(I32), in_=y_codes[:].bitcast(I32)
-            )
-            if cols.stop % R == 0:
-                store_scales(cols.stop - R, cols.stop)
-
-        def live(s):
-            return 0 <= s < STEPS
-
-        def quantize_node(s):
-            st["nq", s] = quantize(work, "node", st["nin", s], PAIR * P)
-
-        def quantize_inputs(s):
-            st["xq", s] = quantize(work, "child", st["xin", s], 2 * PAIR * P)
-
-        def planes_if_whole(s):
-            g, j0 = steps[s]
-            if j0 + PAIR == groups[g][1]:
-                planes_out(g)
-
-        def turns(fresh, results, nodes):
-            for s in fresh:
-                turn_inputs(s)
-            for s in results:
-                turn_sorted("ybf", s)
-            for s in nodes:
-                turn_sorted("node", s)
-            for s in fresh:
-                copy_inputs(s)
-            for s in results:
-                copy_y(s)
-            for s in nodes:
-                copy_node(s)
-
-        def some(s):
-            return [s] if live(s) else []
-
-        for s in range(LEAD):
-            turns([s], [], [])
-            quantize_inputs(s)
-        for s in range(STEPS - LEAD):
-            load_ahead(s)
-            if s > 0:
-                turns([s + LEAD], some(s - LAG_Y), some(s - LAG_N))
-            for r in some(s - LAG_U):
-                stem_products(r)
-            child_products(s)
-            copy_b(s)
-            if s == 0:
-                turns([s + LEAD], [], [])
-            for r in some(s - LAG_U):
-                result(r)
-            node_product(s)
-            for r in some(s - LAG_N):
-                quantize_node(r)
-            for r in some(s - LAG_Y):
-                planes_if_whole(r)
-            quantize_inputs(s + LEAD)
-            for r in some(s - LAG_U):
-                round_pair(r, s + LEAD)
-
-        def turn_node(s):
-            turn_sorted("node", s)
-            copy_node(s)
+                y_tile = work.tile([P, S], BF16)
+                copy(out=write_sorted(y_tile[:]), in_=read_sorted(y[g][:, j0 + j, :]))
+                y_sorted[s, j] = y_tile[:].bitcast(F32).rearrange("p (u m) -> p u m", u=2)
 
         def turn_result(s):
-            turn_sorted("ybf", s)
-            copy_y(s)
+            g, j0 = steps[s]
+            n = groups[g][1]
+            b = turn(lambda j, u: y_sorted[s, j][:, u, :])
+            if j0 == 0:
+                y_turned[g] = work.tile([P, n * S], BF16, name="y_turned", align_bytes=64)
+            words = y_turned[g][:].bitcast(F32).rearrange("p (c i j u) -> p c j u i", i=2, j=n, u=2)
+            nc.scalar.copy(
+                out=words[:, :, j0 : j0 + PAIR],
+                in_=b[:].rearrange("p (u j c i) -> p c j u i", u=2, j=PAIR, i=2),
+            )
+
+        def store_planes(s):
+            g, j0 = steps[s]
+            site0, n = groups[g]
+            if j0 + PAIR < n:
+                return
+            end = site0 + n * P
+            y_codes = keep.tile([P, n * P], U32, name="y_codes_%d" % g, align_bytes=64)
+            nc.vector.quantize_mx(out=y_codes[:].bitcast(FP8X4), scales=y_scales[:, site0:end], in_=y_turned[g][:])
+            nc.sync.dma_start(
+                out=out_1[0, :, site0:end, :].rearrange("p m t -> p (m t)").bitcast(I32), in_=y_codes[:].bitcast(I32)
+            )
+            if end % R == 0:
+                for r in range(4):
+                    queue = nc.scalar if end == C * R and r % 2 else nc.sync
+                    queue.dma_start(
+                        out=out_2[0, r:SCALE_ROWS:4, end - R : end].bitcast(I32),
+                        in_=y_scales[r:P:QUADRANT, end - R : end].bitcast(I32),
+                    )
+
+        for s in range(INPUT_LEAD):
+            turn_children(s)
+            quantize_children(s)
+
+        for s in range(STEPS - INPUT_LEAD):
+            preload(s)
+            child_products(s)
+            for r in if_step(s - STEM_LAG):
+                stem_products(r)
+            copy_b(s)
+            multiply_children(s)
+            for r in if_step(s - STEM_LAG):
+                result(r)
+            for r in if_step(s - NODE_QUANT_LAG):
+                quantize_node(r)
+            for r in if_step(s - PLANES_LAG):
+                store_planes(r)
+            for r in if_step(s - NODE_TURN_LAG):
+                turn_node(r)
+            turn_children(s + INPUT_LEAD)
+            for r in if_step(s - RESULT_TURN_LAG):
+                turn_result(r)
+            quantize_children(s + INPUT_LEAD)
+            for r in if_step(s - STEM_LAG):
+                round_on_gpsimd(r, s + INPUT_LEAD)
 
         last = STEPS - 1
         child_products(last - 1)
+        stem_products(last - 4)
         copy_b(last - 1)
-        stem_products(last - 3)
+        multiply_children(last - 1)
+        result(last - 4)
         turn_node(last - 2)
-        turn_result(last - 5)
-        node_product(last - 1)
+        turn_result(last - 6)
         child_products(last)
         copy_b(last)
-        quantize_node(last - 2)
-        result(last - 3)
+        multiply_children(last)
         turn_node(last - 1)
-        turn_result(last - 4)
-        round_tiles(last - 3, TAILCONV[0])
-        stem_products(last - 2)
-        node_product(last)
+        round_by_copy(last - 4, nc.scalar.copy)
+        turn_result(last - 5)
         turn_node(last)
+        quantize_node(last - 3)
+        quantize_node(last - 2)
+        store_planes(last - 6)
+        stem_products(last - 3)
+        stem_products(last - 2)
+        turn_result(last - 4)
         quantize_node(last - 1)
         stem_products(last - 1)
-        planes_if_whole(last - 4)
-        result(last - 2)
-        turn_result(last - 3)
-        round_tiles(last - 2, TAILCONV[1])
+        result(last - 3)
         quantize_node(last)
+        store_planes(last - 4)
+        round_by_copy(last - 3, nc.scalar.copy)
         stem_products(last)
+        result(last - 2)
+        round_by_copy(last - 2, nc.scalar.copy)
+        turn_result(last - 3)
         result(last - 1)
-        turn_result(last - 2)
-        round_tiles(last - 1, TAILCONV[2])
+        round_by_copy(last - 1, nc.scalar.copy)
         result(last)
+        turn_result(last - 2)
+        round_by_copy(last, nc.vector.tensor_copy)
         turn_result(last - 1)
-        planes_if_whole(last - 3)
-        round_tiles(last, TAILCONV[3])
         turn_result(last)
-        for s in range(last - 2, STEPS):
-            planes_if_whole(s)
+        for s in range(last - 3, STEPS):
+            store_planes(s)

from contextlib import ExitStack

import concourse.mybir as mybir
from concourse.masks import make_identity

C, R, S = 4, 1024, 512
FLOPS = 3 * 2 * C * R * S * S

F32 = mybir.dt.float32
BF16 = mybir.dt.bfloat16
I32 = mybir.dt.int32
U32 = mybir.dt.uint32
U8 = mybir.dt.uint8
FP8X4 = mybir.dt.float8_e4m3fn_x4
FP4X4 = mybir.dt.float4_e2m1fn_x4
MULT = mybir.AluOpType.mult
ADD = mybir.AluOpType.add

P = 128
WORDS = S // 2
PAIR = 2
STEPS = C * R // (PAIR * P)
BANKS = 8
SCALE_ROWS = 16
QUADRANT = 32

WIDE = 4
NARROW_HEAD = 2
NARROW_TAIL = 4

INPUT_LEAD = 2
NODE_TURN_LAG = 1
NODE_QUANT_LAG = 2
STEM_LAG = 3
RESULT_TURN_LAG = 5
PLANES_LAG = 6
CHILD_PRELOAD = 6
SISTER_PRELOAD = 2

FIRST_GROUPS = 4
ROW_BUFS = 5
SHARED_SLOTS = 4


def tile_pruning_rate_categories_k7_kernel(
    tc, left, right, left_words, left_scales, right_words, right_scales,
    stem_words, stem_scales, sister, rescale, out_0, out_1, out_2,
):
    nc = tc.nc

    groups = []
    site = 0
    while site < C * R:
        narrow = site < NARROW_HEAD * PAIR * P or site >= C * R - NARROW_TAIL * PAIR * P
        groups.append((site, PAIR if narrow else WIDE))
        site = site + groups[-1][1] * P
    steps = [(g, j0) for g in range(len(groups)) for j0 in range(0, groups[g][1], PAIR)]
    first_step = [steps.index((g, 0)) for g in range(len(groups))]

    def category(s):
        return groups[steps[s][0]][0] // R

    def group_rows(x, g):
        site0, n = groups[g]
        return x[site0 // R, site0 % R : site0 % R + n * P, :].rearrange("(p j) k -> p j k", j=n)

    def if_step(s):
        return [s] if 0 <= s < STEPS else []

    with ExitStack() as ctx:
        keep = ctx.enter_context(tc.tile_pool(name="keep", bufs=1))
        work = ctx.enter_context(tc.tile_pool(name="work", bufs=4))
        psum = ctx.enter_context(tc.psum_pool(name="psum", bufs=1))
        ctx.enter_context(tc.manual_schedule())

        bank_uses = []

        def next_bank():
            tag = "bank%d" % (len(bank_uses) % BANKS)
            bank_uses.append(tag)
            return psum.tile([P, S], F32, name=tag, tag=tag)

        weight_scales = {}
        for branch in ("right", "left", "stem"):
            weight_scales[branch] = keep.tile([P, C, S], U8, name="scales_" + branch, align_bytes=64)
            nc.vector.memset(weight_scales[branch][:].bitcast(I32), 0)

        ident = keep.tile([P, P], F32)
        make_identity(nc, ident[:])

        def load_scales(branch, src):
            for r in range(4):
                nc.sync.dma_start(
                    out=weight_scales[branch][r:P:QUADRANT, :, :].bitcast(I32),
                    in_=src[:, r:SCALE_ROWS:4, :].rearrange("c q n -> q c n").bitcast(I32),
                )

        weight_words = {}

        def load_words(branch, src, c0, c1):
            w = keep.tile([P, c1 - c0, 2 * S], U8, name="words_%s_%d" % (branch, c0), align_bytes=64)
            nc.sync.dma_start(out=w[:].bitcast(I32), in_=src[c0:c1].rearrange("c p n -> p c n").bitcast(I32))
            for c in range(c0, c1):
                weight_words[branch, c] = w[:, c - c0, :]

        rows = {}

        def load_rows(name, src, g):
            rows[name, g] = work.tile([P, groups[g][1], S], BF16, name="rows_" + name, bufs=ROW_BUFS)
            nc.sync.dma_start(out=rows[name, g][:], in_=group_rows(src, g))

        def load_children(g):
            load_rows("right", right, g)
            load_rows("left", left, g)

        site_factor = {}

        def load_site_factor(n):
            site_factor[n] = keep.tile([P, R // (n * P), n], BF16, name="site_factor_%d" % n)
            nc.sync.dma_start(out=site_factor[n][:], in_=rescale.rearrange("(h p j) -> p h j", p=P, j=n))

        def preload(s):
            for g in range(len(groups)):
                if g >= FIRST_GROUPS and first_step[g] == s + CHILD_PRELOAD:
                    load_children(g)
                if g > 0 and first_step[g] == s + SISTER_PRELOAD:
                    load_rows("sister", sister, g)

        load_children(0)
        load_scales("right", right_scales)
        load_words("right", right_words, 0, 1)
        load_words("left", left_words, 0, 1)
        load_children(1)
        load_scales("left", left_scales)
        load_children(2)
        load_words("stem", stem_words, 0, 1)
        load_scales("stem", stem_scales)
        load_children(3)
        load_site_factor(PAIR)
        load_rows("sister", sister, 0)
        load_words("right", right_words, 1, C)
        load_words("left", left_words, 1, C)
        load_site_factor(WIDE)
        load_words("stem", stem_words, 1, C)
        for s in range(-CHILD_PRELOAD, 0):
            preload(s)

        def read_sorted(ap):
            return ap.rearrange("p (m u e) -> p u m e", u=2, e=2)

        def write_sorted(ap):
            return ap.rearrange("p (u m e) -> p u m e", u=2, e=2)

        def turn(words_of):
            b = next_bank()
            for j in range(PAIR):
                for u in range(2):
                    slot = PAIR * u + j
                    nc.tensor.transpose(b[:, slot * P : (slot + 1) * P], words_of(j, u), ident[:])
            return b

        def interleave(dst, b):
            nc.scalar.copy(
                out=dst.bitcast(F32).rearrange("p (c i u) -> p c u i", i=2, u=2),
                in_=b[:].rearrange("p (u c i) -> p c u i", u=2, i=2),
            )

        def shared_slot(name, width, s):
            return work.tile([P, width], BF16, name=name, tag="shared%d" % (s % SHARED_SLOTS), bufs=1, align_bytes=64)

        def quantize(name, src):
            width = src.shape[1] // 4
            codes = work.tile([P, width], U32, name=name + "_codes", align_bytes=64)
            scales = work.tile([P, width], U8, name=name + "_scales", align_bytes=64)
            nc.vector.quantize_mx(out=codes[:].bitcast(FP8X4), scales=scales[:], in_=src[:])
            return codes, scales

        def product(quantized, slot, branch, c):
            codes, scales = quantized
            b = next_bank()
            nc.tensor.matmul_mx(
                out=b[:],
                lhsT=codes[:, slot * P : (slot + 1) * P].bitcast(FP8X4),
                lhsT_scale=scales[:, slot * P : (slot + 1) * P],
                rhs=weight_words[branch, c].bitcast(FP4X4),
                rhs_scale=weight_scales[branch][:, c, :],
                start=True,
                stop=True,
            )
            return b

        children_turned, children_mx, a_bank, b_bank, b_copy = {}, {}, {}, {}, {}
        node_sorted, node_turned, node_mx, up_bank = {}, {}, {}, {}
        y, y_sorted, y_turned = {}, {}, {}
        y_scales = keep.tile([P, C * R], U8, align_bytes=64)

        def turn_children(s):
            g, j0 = steps[s]
            banks = [
                turn(lambda j, u: rows[name, g][:, j0 + j, :].bitcast(F32)[:, u:WORDS:2]) for name in ("right", "left")
            ]
            children_turned[s] = shared_slot("children_turned", 2 * PAIR * S, s)
            for half in range(2):
                interleave(children_turned[s][:, half * PAIR * S : (half + 1) * PAIR * S], banks[half])

        def quantize_children(s):
            children_mx[s] = quantize("children", children_turned[s])

        def child_products(s):
            for j in range(PAIR):
                b_bank[s, j] = product(children_mx[s], j, "right", category(s))
            for j in range(PAIR):
                a_bank[s, j] = product(children_mx[s], PAIR + j, "left", category(s))

        def copy_b(s):
            for j in range(PAIR):
                b_copy[s, j] = work.tile([P, S], F32, name="b_copy")
                nc.scalar.copy(out=write_sorted(b_copy[s, j][:]), in_=read_sorted(b_bank[s, j][:]))

        def multiply_children(s):
            for j in range(PAIR):
                node = work.tile([P, S], BF16)
                nc.vector.tensor_tensor(
                    out=write_sorted(node[:]), in0=read_sorted(a_bank[s, j][:]), in1=write_sorted(b_copy[s, j][:]), op=MULT
                )
                node_sorted[s, j] = node[:].bitcast(F32).rearrange("p (u m) -> p u m", u=2)

        def turn_node(s):
            b = turn(lambda j, u: node_sorted[s, j][:, u, :])
            node_turned[s] = work.tile([P, PAIR * S], BF16, name="node_turned", align_bytes=64)
            interleave(node_turned[s][:], b)

        def quantize_node(s):
            node_mx[s] = quantize("node", node_turned[s])

        def stem_products(s):
            for j in range(PAIR):
                up_bank[s, j] = product(node_mx[s], j, "stem", category(s))

        def result(s):
            g, j0 = steps[s]
            site0, n = groups[g]
            if j0 == 0:
                y[g] = keep.tile([P, n, S], F32, name="y_%d" % g)
            for j in range(j0, j0 + PAIR):
                nc.vector.scalar_tensor_tensor(
                    out=y[g][:, j, :],
                    in0=up_bank[s, j - j0][:],
                    scalar=site_factor[n][:, site0 % R // (n * P), j : j + 1],
                    in1=rows["sister", g][:, j, :],
                    op0=MULT,
                    op1=MULT,
                )
            if j0 + PAIR == n:
                nc.sync.dma_start(out=group_rows(out_0, g), in_=y[g][:])

        def round_on_gpsimd(s, slot_step):
            g, j0 = steps[s]
            pair = shared_slot("y_pair", PAIR * S, slot_step)
            nc.gpsimd.tensor_scalar(
                out=pair[:].rearrange("p (u w e) -> p u w e", u=2, e=2),
                in0=y[g][:, j0 : j0 + PAIR, :].rearrange("p j (m u e) -> p u (j m) e", u=2, e=2),
                scalar1=1.0,
                scalar2=0.0,
                op0=MULT,
                op1=ADD,
            )
            for j in range(PAIR):
                y_sorted[s, j] = pair[:].bitcast(F32).rearrange("p (u j m) -> p j u m", u=2, j=PAIR)[:, j]

        def round_by_copy(s, copy):
            g, j0 = steps[s]
            for j in range(PAIR):
                y_tile = work.tile([P, S], BF16)
                copy(out=write_sorted(y_tile[:]), in_=read_sorted(y[g][:, j0 + j, :]))
                y_sorted[s, j] = y_tile[:].bitcast(F32).rearrange("p (u m) -> p u m", u=2)

        def turn_result(s):
            g, j0 = steps[s]
            n = groups[g][1]
            b = turn(lambda j, u: y_sorted[s, j][:, u, :])
            if j0 == 0:
                y_turned[g] = work.tile([P, n * S], BF16, name="y_turned", align_bytes=64)
            words = y_turned[g][:].bitcast(F32).rearrange("p (c i j u) -> p c j u i", i=2, j=n, u=2)
            nc.scalar.copy(
                out=words[:, :, j0 : j0 + PAIR],
                in_=b[:].rearrange("p (u j c i) -> p c j u i", u=2, j=PAIR, i=2),
            )

        def store_planes(s):
            g, j0 = steps[s]
            site0, n = groups[g]
            if j0 + PAIR < n:
                return
            end = site0 + n * P
            y_codes = keep.tile([P, n * P], U32, name="y_codes_%d" % g, align_bytes=64)
            nc.vector.quantize_mx(out=y_codes[:].bitcast(FP8X4), scales=y_scales[:, site0:end], in_=y_turned[g][:])
            nc.sync.dma_start(
                out=out_1[0, :, site0:end, :].rearrange("p m t -> p (m t)").bitcast(I32), in_=y_codes[:].bitcast(I32)
            )
            if end % R == 0:
                for r in range(4):
                    queue = nc.scalar if end == C * R and r % 2 else nc.sync
                    queue.dma_start(
                        out=out_2[0, r:SCALE_ROWS:4, end - R : end].bitcast(I32),
                        in_=y_scales[r:P:QUADRANT, end - R : end].bitcast(I32),
                    )

        for s in range(INPUT_LEAD):
            turn_children(s)
            quantize_children(s)

        for s in range(STEPS - INPUT_LEAD):
            preload(s)
            child_products(s)
            for r in if_step(s - STEM_LAG):
                stem_products(r)
            copy_b(s)
            multiply_children(s)
            for r in if_step(s - STEM_LAG):
                result(r)
            for r in if_step(s - NODE_QUANT_LAG):
                quantize_node(r)
            for r in if_step(s - PLANES_LAG):
                store_planes(r)
            for r in if_step(s - NODE_TURN_LAG):
                turn_node(r)
            turn_children(s + INPUT_LEAD)
            for r in if_step(s - RESULT_TURN_LAG):
                turn_result(r)
            quantize_children(s + INPUT_LEAD)
            for r in if_step(s - STEM_LAG):
                round_on_gpsimd(r, s + INPUT_LEAD)

        last = STEPS - 1
        child_products(last - 1)
        stem_products(last - 4)
        copy_b(last - 1)
        multiply_children(last - 1)
        result(last - 4)
        turn_node(last - 2)
        turn_result(last - 6)
        child_products(last)
        copy_b(last)
        multiply_children(last)
        turn_node(last - 1)
        round_by_copy(last - 4, nc.scalar.copy)
        turn_result(last - 5)
        turn_node(last)
        quantize_node(last - 3)
        quantize_node(last - 2)
        store_planes(last - 6)
        stem_products(last - 3)
        stem_products(last - 2)
        turn_result(last - 4)
        quantize_node(last - 1)
        stem_products(last - 1)
        result(last - 3)
        quantize_node(last)
        store_planes(last - 4)
        round_by_copy(last - 3, nc.scalar.copy)
        stem_products(last)
        result(last - 2)
        round_by_copy(last - 2, nc.scalar.copy)
        turn_result(last - 3)
        result(last - 1)
        round_by_copy(last - 1, nc.scalar.copy)
        result(last)
        turn_result(last - 2)
        round_by_copy(last, nc.vector.tensor_copy)
        turn_result(last - 1)
        turn_result(last)
        for s in range(last - 3, STEPS):
            store_planes(s)
